import numpy as np
import ml_dtypes


def mxq(x, axis, fmt="e4m3"):
    dtype, down = {"e4m3": (ml_dtypes.float8_e4m3fn, 7), "e5m2": (ml_dtypes.float8_e5m2, 14)}[fmt]
    v = np.moveaxis(np.asarray(x, np.float32).astype(ml_dtypes.bfloat16).astype(np.float64), axis, -1)
    blocks = v.reshape(v.shape[:-1] + (-1, 32))
    amax = np.abs(blocks).max(-1, keepdims=True)
    byte = np.maximum(np.where(amax > 0, np.frexp(amax)[1] - 1 + 127, 0) - down, 1)
    scale = np.exp2(byte - 127.0)
    codes = (blocks / scale).astype(np.float32).astype(dtype).astype(np.float64)
    return np.moveaxis((codes * scale).reshape(v.shape), -1, axis)


WIDE = False


def mx_kscale(k):
    if not WIDE:
        return np.ones(k)
    levels = np.array([10, -10, 5, -5, 0])
    if k % 512:
        return np.exp2(np.random.permutation(np.resize(levels, k // 32))).repeat(32)
    a = np.empty((k // 512, 16))
    for p in range(k // 512):
        a[p, :8] = np.random.permutation(np.resize(levels, 8))
        for g in range(8):
            far = levels[np.abs(levels - a[p, g]) >= 10]
            a[p, g + 8] = far[np.random.randint(len(far))]
    return np.exp2(a.ravel()).repeat(32)


def f64(x):
    return np.asarray(x).astype(np.float64)


def striped(idx):
    return np.tile(idx.reshape(-1, 16).T, (8, 1)).astype(np.uint16)


def unstriped(offs):
    return offs[:16].T.reshape(-1).astype(np.int64)


def pack_weight(w):
    k, n = w.shape
    w = f64(np.asarray(w, np.float32).astype(ml_dtypes.bfloat16)).reshape(k // 32, 32, n)
    amax = np.abs(w).max(1)
    byte = np.clip(np.where(amax > 0, np.frexp(amax)[1] - 1 + 127 - 7, 1), 1, 254)
    scaled = (w * np.exp2(127.0 - byte)[:, None, :]).reshape(k, n).astype(np.float32)
    words = np.ascontiguousarray(scaled.reshape(k // 512, 128, 4, n).transpose(0, 1, 3, 2)).astype(ml_dtypes.float8_e4m3fn).view(np.uint8)
    return words, np.ascontiguousarray(byte.astype(np.uint8).reshape(k // 512, 16, n))


def unpack_weight(words, scales):
    g, p, n, _ = words.shape
    vals = np.ascontiguousarray(words).view(ml_dtypes.float8_e4m3fn).astype(np.float64) * np.repeat(np.exp2(scales.astype(np.float64) - 127.0), 8, axis=1)[..., None]
    return vals.transpose(0, 1, 3, 2).reshape(g * 512, n)


def sigmoid(v):
    return 1.0 / (1.0 + np.exp(-np.maximum(v, -700.0)))


K, T, S, D, N = 512, 2048, 512, 4, 256
P = 2 ** 7


def setup_inputs():
    n = np.random.standard_normal
    s = mx_kscale(K)[:, None]
    packed_xT = pack_weight(n((K, T)) * s)
    return {
        "x_words": packed_xT[0],
        "x_scales": packed_xT[1],
        "w1": (n((K, N)) / np.sqrt(K) / s).astype(np.float32),
        "w2": (n((K, N)) / np.sqrt(K) / s).astype(np.float32),
        "w3": (n((K, N)) / np.sqrt(K) / s).astype(np.float32),
        "light": (np.tile(np.random.uniform(2.0, 9.0, S), (P, 1))).astype(np.float32),
        "wim": (np.random.uniform(0.2, 0.8, (N, 1))).astype(np.float32),
        "offs": striped(np.random.permutation(T)[:S]),
    }


def reference(x_words, x_scales, w1, w2, w3, light, wim, offs):
    xq = unpack_weight(x_words, x_scales)[:, unstriped(offs)]
    yv = mxq(f64(w1), 0, "e4m3").T @ xq
    vcm = 0.8 * (np.log(np.exp(yv) + 1.0)) + 0.2
    yc = mxq(f64(w3), 0, "e4m3").T @ xq
    ci = 1.2 * sigmoid(yc) + 0.4
    cg = ci - 0.1
    wc = (vcm * cg) / (ci + 0.7)
    yj = mxq(f64(w2), 0, "e4m3").T @ xq
    jmx = 2.0 * (np.log(np.exp(yj) + 1.0)) + 1.5
    lj = f64(light)[:1] + jmx
    jel = 0.714286 * (lj - (np.sqrt((lj) ** 2 - (2.8 * (f64(light)[:1] * jmx)))))
    wj = (jel * cg) / (4.0 * ci + 0.8)
    net = np.minimum(wc, wj) - (0.05 * vcm)
    cond = net / (ci + 0.3)
    imb = np.abs(wc - wj)
    return cond.reshape(len(cond), -1, D).mean(axis=2) + f64(wim) * (imb.reshape(len(imb), -1, D).max(axis=2))

@@ -1,0 +1,238 @@
+import math
+from contextlib import ExitStack
+
+import concourse.mybir as mybir
+from concourse.masks import make_identity
+
+F32 = mybir.dt.float32
+BF16 = mybir.dt.bfloat16
+I32 = mybir.dt.int32
+U32 = mybir.dt.uint32
+U16 = mybir.dt.uint16
+U8 = mybir.dt.uint8
+FP8X4 = mybir.dt.float8_e4m3fn_x4
+ACT = mybir.ActivationFunctionType
+ALU = mybir.AluOpType
+
+P = 128
+K, T, S, D, N = 512, 2048, 512, 4, 256
+PACK = 4
+HALVES = N // P
+FLOPS = 3 * 2 * K * N * S
+
+SLOPE = 0.714286
+SHIFT = 0.25
+EXP_CAP = 2.0**60
+
+HALF_LOG_A = 0.5 * math.log(2.3 / 1.1)
+HALF_LOG_B = 0.5 * math.log(7.2 / 2.4)
+HALF_LOG_C = 0.5 * math.log(1.9 / 0.7)
+INV_A_SLOPE = 0.6 / (1.1 * 2.3)
+RATIO_SCALE = (0.4 / SLOPE) * 2.0 * INV_A_SLOPE
+RATIO_SHIFT = 1.0 + (4.0 - 2.0 / 1.1) / (2.0 * INV_A_SLOPE)
+DIFF_UNIT = SLOPE / 12.0
+INV_C_SLOPE = 0.6 / (0.7 * 1.9)
+CUT_UNIT = -DIFF_UNIT / D
+GAIN_SHIFT = 1.0 + (0.95 - 0.8 / 1.1) / (0.8 * INV_A_SLOPE)
+GAIN_SCALE = (0.8 / D) * (0.8 * INV_A_SLOPE) / CUT_UNIT
+
+
+def tile_picked_yfarqu_cond_p_kernel(
+    tc, x_words, x_scales, w1, w2, w3, light, wim, offs, out
+):
+    nc = tc.nc
+    with ExitStack() as ctx:
+        keep = ctx.enter_context(tc.tile_pool(name="keep", bufs=1))
+        psum = ctx.enter_context(tc.psum_pool(name="psum", bufs=1))
+
+        offsets = keep.tile([P, S // 16], U16, name="offsets")
+        nc.sync.dma_start(offsets[:], offs)
+
+        scale_table = keep.tile([P, T], U8, name="scale_table", align_bytes=64)
+        nc.vector.memset(scale_table[:].bitcast(I32), 0)
+
+        def load_weight(name, columns):
+            raw = keep.tile([P, PACK, columns.shape[1]], F32, name=name)
+            nc.sync.dma_start(raw[:], columns.rearrange("(p j) m -> p j m", j=PACK))
+            return raw
+
+        w3_raw = [load_weight("w3_raw0", w3[:, 0:P])]
+        for q in range(4):
+            nc.sync.dma_start(
+                scale_table[32 * q : 32 * q + 4, :].bitcast(I32),
+                x_scales[0, 4 * q : 4 * q + 4, :].bitcast(I32),
+            )
+        word_table = keep.tile([P, T], I32, name="word_table", align_bytes=64)
+        nc.sync.dma_start(word_table[:], x_words[0].rearrange("p c r -> p (c r)").bitcast(I32))
+        w3_raw.append(load_weight("w3_raw1", w3[:, P:N]))
+        w2_raw = load_weight("w2_raw", w2)
+        w1_raw = load_weight("w1_raw", w1)
+        light_col = keep.tile([P, D], F32, name="light_col")
+        nc.sync.dma_start(light_col[:], light[0].rearrange("(p t) -> p t", t=D))
+        wim_col = keep.tile([P, HALVES], F32, name="wim_col")
+        with nc.allow_non_contiguous_dma(reason="one weight for each output row"):
+            nc.sync.dma_start(wim_col[:], wim.rearrange("(h p) o -> p (h o)", p=P))
+
+        ident = keep.tile([P, P], F32, name="ident")
+        make_identity(nc, ident[:])
+
+        w3_grouped, w3_codes, w3_scales = [], [], []
+        for h in range(HALVES):
+            w3_grouped.append(keep.tile([P, P, PACK], BF16, name="w3_grouped%d" % h, align_bytes=64))
+            w3_codes.append(keep.tile([P, P], U32, name="w3_codes%d" % h, align_bytes=64))
+            w3_scales.append(keep.tile([P, P], U8, name="w3_scales%d" % h, align_bytes=64))
+            nc.scalar.copy(w3_grouped[h][:], w3_raw[h][:].rearrange("p j m -> p m j"))
+
+        def quantize(grouped, codes, scales):
+            nc.vector.quantize_mx(
+                out=codes.bitcast(FP8X4), scales=scales, in_=grouped[:].rearrange("p m j -> p (m j)")
+            )
+
+        picked_scales = keep.tile([P, S], U8, name="picked_scales", align_bytes=64)
+        nc.vector.tensor_copy(picked_scales[:], scale_table[:].indirect(offsets[:]))
+        quantize(w3_grouped[0], w3_codes[0][:], w3_scales[0][:])
+        x_scale = keep.tile([P, D, P], U8, name="x_scale", align_bytes=64)
+        nc.vector.tensor_copy(
+            x_scale[:].rearrange("q t p -> q p t"), picked_scales[:].rearrange("q (p t) -> q p t", t=D)
+        )
+        x_code = keep.tile([P, D, P], U32, name="x_code", align_bytes=64)
+        nc.vector.tensor_copy(
+            x_code[:].rearrange("q t p -> q p t"), word_table[:].bitcast(U32).indirect(offsets[:])
+        )
+        quantize(w3_grouped[1], w3_codes[1][:], w3_scales[1][:])
+
+        def product(acc, t, codes, scales):
+            nc.tensor.matmul_mx(
+                out=acc,
+                lhsT=x_code[:, t, :].bitcast(FP8X4),
+                lhsT_scale=x_scale[:, t, :],
+                rhs=codes.bitcast(FP8X4),
+                rhs_scale=scales,
+                start=True,
+                stop=True,
+            )
+
+        yc = [psum.tile([P, D, P], F32, name="yc%d" % h) for h in range(HALVES)]
+        tanh_a = keep.tile([P, D, N], F32, name="tanh_a")
+        tanh_b = keep.tile([P, D, N], F32, name="tanh_b")
+        tanh_c = keep.tile([P, D, N], F32, name="tanh_c")
+        for h in range(HALVES):
+            for t in range(D):
+                product(yc[h][:, t, :], t, w3_codes[h][:], w3_scales[h][:])
+            for dst, half_log in ((tanh_c, HALF_LOG_C), (tanh_a, HALF_LOG_A), (tanh_b, HALF_LOG_B)):
+                nc.scalar.activation(
+                    dst[:, :, h * P : (h + 1) * P], yc[h][:], ACT.Tanh, bias=half_log, scale=0.5
+                )
+
+        jv_codes = keep.tile([P, 2 * N], U32, name="jv_codes", align_bytes=64)
+        jv_scales = keep.tile([P, 2 * N], U8, name="jv_scales", align_bytes=64)
+        for i, raw in enumerate((w2_raw, w1_raw)):
+            grouped = keep.tile([P, N, PACK], BF16, name="jv_grouped%d" % i, align_bytes=64)
+            nc.vector.tensor_copy(grouped[:], raw[:].rearrange("p j m -> p m j"))
+            quantize(grouped, jv_codes[:, i * N : (i + 1) * N], jv_scales[:, i * N : (i + 1) * N])
+
+        centre = keep.tile([P, D], F32, name="centre")
+        lift = keep.tile([P, D], F32, name="lift")
+        light_part = keep.tile([P, D], F32, name="light_part")
+        floor = keep.tile([P, D], F32, name="floor")
+        nc.gpsimd.tensor_scalar(centre[:], light_col[:], -0.2, 0.75 - SHIFT, ALU.mult, ALU.add)
+        nc.gpsimd.tensor_scalar(lift[:], light_col[:], 0.5, 0.75 - SHIFT, ALU.mult, ALU.add)
+        nc.gpsimd.tensor_scalar(light_part[:], light_col[:], 0.21, 0.0, ALU.mult, ALU.add)
+        nc.gpsimd.tensor_tensor(floor[:], light_part[:], light_col[:], ALU.mult)
+
+        yjv = [psum.tile([P, 2 * N], F32, name="yjv%d" % t) for t in range(D)]
+        grown = keep.tile([P, D, 2 * N], F32, name="grown")
+        for t in range(D):
+            product(yjv[t][:], t, jv_codes[:], jv_scales[:])
+            nc.scalar.activation(grown[:, t, :], yjv[t][:], ACT.Exp)
+
+        cut = keep.tile([P, D, N], F32, name="cut")
+        nc.vector.tensor_scalar(
+            cut[:], tanh_c[:], -INV_C_SLOPE * CUT_UNIT, (1.0 / 0.7 - INV_C_SLOPE) * CUT_UNIT, ALU.mult, ALU.add
+        )
+        gain = keep.tile([P, D, N], F32, name="gain")
+        nc.vector.scalar_tensor_tensor(gain[:], tanh_a[:], GAIN_SHIFT, cut[:], ALU.add, ALU.mult)
+
+        pairs = [slice(0, 2), slice(2, 4)]
+        for pair in pairs:
+            nc.vector.tensor_scalar_min(grown[:, pair, :], grown[:, pair, :], EXP_CAP)
+
+        logs = keep.tile([P, D, 2 * N], F32, name="logs")
+        soft = keep.tile([P, D, 2 * N], F32, name="soft")
+        for t in range(D):
+            nc.scalar.activation(
+                logs[:, t, :], grown[:, t, :], ACT.Ln, bias=math.exp(SHIFT), scale=math.exp(SHIFT)
+            )
+        for t in range(D):
+            nc.vector.scalar_tensor_tensor(soft[:, t, :], yjv[t][:], SHIFT, logs[:, t, :], ALU.add, ALU.max)
+        soft_j = soft[:, :, 0:N]
+        soft_v = soft[:, :, N : 2 * N]
+
+        square = keep.tile([P, D, N], F32, name="square")
+        root = keep.tile([P, D, N], F32, name="root")
+        for t in range(D):
+            nc.scalar.activation(square[:, t, :], soft_j[:, t, :], ACT.Square, bias=centre[:, t : t + 1])
+        for t in range(D):
+            nc.scalar.activation(root[:, t, :], square[:, t, :], ACT.Sqrt, bias=floor[:, t : t + 1])
+
+        ratio_v = keep.tile([P, D, N], F32, name="ratio_v")
+        lead = keep.tile([P, D, N], F32, name="lead")
+        base = keep.tile([P, D, N], F32, name="base")
+        for pair in pairs:
+            nc.vector.scalar_tensor_tensor(
+                ratio_v[:, pair, :], tanh_a[:, pair, :], RATIO_SHIFT, soft_v[:, pair, :], ALU.add, ALU.mult
+            )
+        for pair in pairs:
+            nc.vector.scalar_tensor_tensor(
+                lead[:, pair, :], ratio_v[:, pair, :], RATIO_SCALE, soft_j[:, pair, :], ALU.mult, ALU.subtract
+            )
+        for pair in pairs:
+            nc.vector.scalar_tensor_tensor(
+                base[:, pair, :], gain[:, pair, :], GAIN_SCALE, soft_v[:, pair, :], ALU.mult, ALU.mult
+            )
+
+        mean = [psum.tile([P, P], F32, name="mean%d" % h) for h in range(HALVES)]
+
+        def add_turned(src, t, start, stop):
+            for h in range(HALVES):
+                nc.tensor.matmul(
+                    mean[h][:], src[:, t, h * P : (h + 1) * P], ident[:], start=start, stop=stop, is_transpose=True
+                )
+
+        for t in range(D):
+            add_turned(base, t, t == 0, False)
+
+        gap = keep.tile([P, D, N], F32, name="gap")
+        diff = keep.tile([P, D, N], F32, name="diff")
+        loss = keep.tile([P, D, N], F32, name="loss")
+        size = keep.tile([P, D, N], F32, name="size")
+        pair_max = keep.tile([P, 2, N], F32, name="pair_max")
+        for t in range(D):
+            nc.vector.scalar_tensor_tensor(
+                gap[:, t, :], root[:, t, :], lift[:, t : t + 1], lead[:, t, :], ALU.subtract, ALU.add
+            )
+        for pair in pairs:
+            nc.vector.scalar_tensor_tensor(
+                diff[:, pair, :], tanh_b[:, pair, :], 4.0, gap[:, pair, :], ALU.add, ALU.mult
+            )
+            nc.scalar.activation(size[:, pair, :], diff[:, pair, :], ACT.Abs, scale=DIFF_UNIT)
+        for pair in pairs:
+            nc.vector.scalar_tensor_tensor(
+                loss[:, pair, :], diff[:, pair, :], 0.0, cut[:, pair, :], ALU.max, ALU.mult
+            )
+            for t in range(pair.start, pair.stop):
+                add_turned(loss, t, False, t == D - 1)
+        for u in range(2):
+            nc.vector.tensor_tensor(pair_max[:, u, :], size[:, 2 * u, :], size[:, 2 * u + 1, :], ALU.max)
+        worst = keep.tile([P, N], F32, name="worst")
+        nc.vector.tensor_tensor(worst[:], pair_max[:, 0, :], pair_max[:, 1, :], ALU.max)
+
+        result = keep.tile([P, HALVES, P], F32, name="result")
+        mean_sb = keep.tile([P, HALVES, P], F32, name="mean_sb")
+        for h in range(HALVES):
+            nc.scalar.copy(mean_sb[:, h, :], mean[h][:])
+            nc.tensor.transpose(yc[h][:, 0, :], worst[:, h * P : (h + 1) * P], ident[:])
+            nc.vector.scalar_tensor_tensor(
+                result[:, h, :], yc[h][:, 0, :], wim_col[:, h : h + 1], mean_sb[:, h, :], ALU.mult, ALU.add
+            )
+        nc.sync.dma_start(out.rearrange("(h p) v -> p h v", p=P), result[:])

@@ -23,6 +23,7 @@ FLOPS = 3 * 2 * K * N * S
 SLOPE = 0.714286
 SHIFT = 0.25
 EXP_CAP = 2.0**60
+FIRST_WORDS = 512
 
 HALF_LOG_A = 0.5 * math.log(2.3 / 1.1)
 HALF_LOG_B = 0.5 * math.log(7.2 / 2.4)
@@ -49,24 +50,25 @@ def tile_picked_yfarqu_cond_p_kernel(
         nc.sync.dma_start(offsets[:], offs)
 
         scale_table = keep.tile([P, T], U8, name="scale_table", align_bytes=64)
-        nc.vector.memset(scale_table[:].bitcast(I32), 0)
+        nc.gpsimd.memset(scale_table[:].bitcast(I32), 0)
 
         def load_weight(name, columns):
-            raw = keep.tile([P, PACK, columns.shape[1]], F32, name=name)
+            raw = keep.tile([P, PACK, columns.shape[1]], F32, name=name, tag=name)
             nc.sync.dma_start(raw[:], columns.rearrange("(p j) m -> p j m", j=PACK))
             return raw
 
-        w3_raw = [load_weight("w3_raw0", w3[:, 0:P])]
+        word_table = keep.tile([P, T], I32, name="word_table", align_bytes=64)
+        words = x_words[0].rearrange("p c r -> p (c r)").bitcast(I32)
+        nc.sync.dma_start(word_table[:, 0:FIRST_WORDS], words[:, 0:FIRST_WORDS])
         for q in range(4):
             nc.sync.dma_start(
                 scale_table[32 * q : 32 * q + 4, :].bitcast(I32),
                 x_scales[0, 4 * q : 4 * q + 4, :].bitcast(I32),
             )
-        word_table = keep.tile([P, T], I32, name="word_table", align_bytes=64)
-        nc.sync.dma_start(word_table[:], x_words[0].rearrange("p c r -> p (c r)").bitcast(I32))
-        w3_raw.append(load_weight("w3_raw1", w3[:, P:N]))
-        w2_raw = load_weight("w2_raw", w2)
+        nc.sync.dma_start(word_table[:, FIRST_WORDS:T], words[:, FIRST_WORDS:T])
+        w3_raw = [load_weight("w3_raw%d" % h, w3[:, h * P : (h + 1) * P]) for h in range(HALVES)]
         w1_raw = load_weight("w1_raw", w1)
+        w2_raw = load_weight("w2_raw", w2)
         light_col = keep.tile([P, D], F32, name="light_col")
         nc.sync.dma_start(light_col[:], light[0].rearrange("(p t) -> p t", t=D))
         wim_col = keep.tile([P, HALVES], F32, name="wim_col")
@@ -78,7 +80,7 @@ def tile_picked_yfarqu_cond_p_kernel(
 
         w3_grouped, w3_codes, w3_scales = [], [], []
         for h in range(HALVES):
-            w3_grouped.append(keep.tile([P, P, PACK], BF16, name="w3_grouped%d" % h, align_bytes=64))
+            w3_grouped.append(keep.tile([P, P, PACK], BF16, name="w3_grouped%d" % h, tag="grouped%d" % h, align_bytes=64))
             w3_codes.append(keep.tile([P, P], U32, name="w3_codes%d" % h, align_bytes=64))
             w3_scales.append(keep.tile([P, P], U8, name="w3_scales%d" % h, align_bytes=64))
             nc.scalar.copy(w3_grouped[h][:], w3_raw[h][:].rearrange("p j m -> p m j"))
@@ -90,16 +92,14 @@ def tile_picked_yfarqu_cond_p_kernel(
 
         picked_scales = keep.tile([P, S], U8, name="picked_scales", align_bytes=64)
         nc.vector.tensor_copy(picked_scales[:], scale_table[:].indirect(offsets[:]))
-        quantize(w3_grouped[0], w3_codes[0][:], w3_scales[0][:])
         x_scale = keep.tile([P, D, P], U8, name="x_scale", align_bytes=64)
-        nc.vector.tensor_copy(
-            x_scale[:].rearrange("q t p -> q p t"), picked_scales[:].rearrange("q (p t) -> q p t", t=D)
-        )
+        nc.vector.tensor_copy(x_scale[:], picked_scales[:].rearrange("q (p t) -> q t p", t=D))
         x_code = keep.tile([P, D, P], U32, name="x_code", align_bytes=64)
         nc.vector.tensor_copy(
             x_code[:].rearrange("q t p -> q p t"), word_table[:].bitcast(U32).indirect(offsets[:])
         )
-        quantize(w3_grouped[1], w3_codes[1][:], w3_scales[1][:])
+        for h in range(HALVES):
+            quantize(w3_grouped[h], w3_codes[h][:], w3_scales[h][:])
 
         def product(acc, t, codes, scales):
             nc.tensor.matmul_mx(
@@ -112,7 +112,7 @@ def tile_picked_yfarqu_cond_p_kernel(
                 stop=True,
             )
 
-        yc = [psum.tile([P, D, P], F32, name="yc%d" % h) for h in range(HALVES)]
+        yc = [psum.tile([P, D, P], F32, name="yc%d" % h, tag="bank_c%d" % h) for h in range(HALVES)]
         tanh_a = keep.tile([P, D, N], F32, name="tanh_a")
         tanh_b = keep.tile([P, D, N], F32, name="tanh_b")
         tanh_c = keep.tile([P, D, N], F32, name="tanh_c")
@@ -124,12 +124,12 @@ def tile_picked_yfarqu_cond_p_kernel(
                     dst[:, :, h * P : (h + 1) * P], yc[h][:], ACT.Tanh, bias=half_log, scale=0.5
                 )
 
-        jv_codes = keep.tile([P, 2 * N], U32, name="jv_codes", align_bytes=64)
-        jv_scales = keep.tile([P, 2 * N], U8, name="jv_scales", align_bytes=64)
-        for i, raw in enumerate((w2_raw, w1_raw)):
-            grouped = keep.tile([P, N, PACK], BF16, name="jv_grouped%d" % i, align_bytes=64)
+        jv_codes = [keep.tile([P, N], U32, name="jv_codes%d" % b, align_bytes=64) for b in range(2)]
+        jv_scales = [keep.tile([P, N], U8, name="jv_scales%d" % b, align_bytes=64) for b in range(2)]
+        for i, raw in enumerate((w1_raw, w2_raw)):
+            grouped = keep.tile([P, N, PACK], BF16, name="jv_grouped%d" % i, tag="grouped%d" % (1 - i), align_bytes=64)
             nc.vector.tensor_copy(grouped[:], raw[:].rearrange("p j m -> p m j"))
-            quantize(grouped, jv_codes[:, i * N : (i + 1) * N], jv_scales[:, i * N : (i + 1) * N])
+            quantize(grouped, jv_codes[i][:], jv_scales[i][:])
 
         centre = keep.tile([P, D], F32, name="centre")
         lift = keep.tile([P, D], F32, name="lift")
@@ -140,13 +140,28 @@ def tile_picked_yfarqu_cond_p_kernel(
         nc.gpsimd.tensor_scalar(light_part[:], light_col[:], 0.21, 0.0, ALU.mult, ALU.add)
         nc.gpsimd.tensor_tensor(floor[:], light_part[:], light_col[:], ALU.mult)
 
-        yjv = [psum.tile([P, 2 * N], F32, name="yjv%d" % t) for t in range(D)]
-        grown = keep.tile([P, D, 2 * N], F32, name="grown")
-        for t in range(D):
-            product(yjv[t][:], t, jv_codes[:], jv_scales[:])
-            nc.scalar.activation(grown[:, t, :], yjv[t][:], ACT.Exp)
+        grown = [keep.tile([P, HALVES, S], F32, name="grown%d" % b) for b in range(2)]
+        excess = [keep.tile([P, HALVES, S], F32, name="excess%d" % b) for b in range(2)]
+        logs = [keep.tile([P, HALVES, S], F32, name="logs%d" % b) for b in range(2)]
+        y = [
+            [psum.tile([P, S], F32, name="y%d%d" % (b, h), tag="bank_y%d%d" % (b, h)) for h in range(HALVES)]
+            for b in range(2)
+        ]
+        for b in range(2):
+            for h in range(HALVES):
+                columns = slice(h * P, (h + 1) * P)
+                nc.tensor.matmul_mx(
+                    out=y[b][h][:],
+                    lhsT=jv_codes[b][:, columns].bitcast(FP8X4),
+                    lhsT_scale=jv_scales[b][:, columns],
+                    rhs=x_code[:].rearrange("q t p -> q (t p)").bitcast(FP8X4),
+                    rhs_scale=x_scale[:].rearrange("q t p -> q (t p)"),
+                    start=True,
+                    stop=True,
+                )
+                nc.scalar.activation(grown[b][:, h, :], y[b][h][:], ACT.Exp)
 
-        cut = keep.tile([P, D, N], F32, name="cut")
+        cut = keep.tile([P, D, N], F32, name="cut", tag="w2_raw")
         nc.vector.tensor_scalar(
             cut[:], tanh_c[:], -INV_C_SLOPE * CUT_UNIT, (1.0 / 0.7 - INV_C_SLOPE) * CUT_UNIT, ALU.mult, ALU.add
         )
@@ -154,44 +169,50 @@ def tile_picked_yfarqu_cond_p_kernel(
         nc.vector.scalar_tensor_tensor(gain[:], tanh_a[:], GAIN_SHIFT, cut[:], ALU.add, ALU.mult)
 
         pairs = [slice(0, 2), slice(2, 4)]
-        for pair in pairs:
-            nc.vector.tensor_scalar_min(grown[:, pair, :], grown[:, pair, :], EXP_CAP)
+        for b in range(2):
+            for h in range(HALVES):
+                nc.vector.tensor_scalar(
+                    excess[b][:, h, :], y[b][h][:], -math.log(EXP_CAP), 0.0, ALU.add, ALU.max
+                )
+            nc.vector.tensor_scalar_min(grown[b][:], grown[b][:], EXP_CAP)
 
-        logs = keep.tile([P, D, 2 * N], F32, name="logs")
-        soft = keep.tile([P, D, 2 * N], F32, name="soft")
-        for t in range(D):
-            nc.scalar.activation(
-                logs[:, t, :], grown[:, t, :], ACT.Ln, bias=math.exp(SHIFT), scale=math.exp(SHIFT)
-            )
-        for t in range(D):
-            nc.vector.scalar_tensor_tensor(soft[:, t, :], yjv[t][:], SHIFT, logs[:, t, :], ALU.add, ALU.max)
-        soft_j = soft[:, :, 0:N]
-        soft_v = soft[:, :, N : 2 * N]
+        soft_tags = [["bank_s0", "bank_c0"], ["bank_s1", "bank_c1"]]
+        soft = [
+            [psum.tile([P, 2, N], F32, name="soft%d%d" % (b, u), tag=soft_tags[b][u]) for u in range(2)]
+            for b in range(2)
+        ]
+
+        def turn_into_soft(src, b, u, opens):
+            for i in range(2):
+                for h in range(HALVES):
+                    t = 2 * u + i
+                    nc.tensor.matmul(
+                        soft[b][u][:, i, h * P : (h + 1) * P],
+                        src[b][:, h, t * P : (t + 1) * P],
+                        ident[:],
+                        start=opens and i == 0 and h == 0,
+                        stop=(not opens) and i == 1 and h == HALVES - 1,
+                        is_transpose=True,
+                    )
+
+        for b in range(2):
+            for u in range(2):
+                turn_into_soft(excess, b, u, True)
+        for u in range(2):
+            for b in range(2):
+                columns = slice(2 * u * P, 2 * (u + 1) * P)
+                nc.scalar.activation(
+                    logs[b][:, :, columns], grown[b][:, :, columns], ACT.Ln, bias=math.exp(SHIFT), scale=math.exp(SHIFT)
+                )
+                turn_into_soft(logs, b, u, False)
+        soft_v, soft_j = soft
 
         square = keep.tile([P, D, N], F32, name="square")
         root = keep.tile([P, D, N], F32, name="root")
-        for t in range(D):
-            nc.scalar.activation(square[:, t, :], soft_j[:, t, :], ACT.Square, bias=centre[:, t : t + 1])
-        for t in range(D):
-            nc.scalar.activation(root[:, t, :], square[:, t, :], ACT.Sqrt, bias=floor[:, t : t + 1])
-
         ratio_v = keep.tile([P, D, N], F32, name="ratio_v")
         lead = keep.tile([P, D, N], F32, name="lead")
         base = keep.tile([P, D, N], F32, name="base")
-        for pair in pairs:
-            nc.vector.scalar_tensor_tensor(
-                ratio_v[:, pair, :], tanh_a[:, pair, :], RATIO_SHIFT, soft_v[:, pair, :], ALU.add, ALU.mult
-            )
-        for pair in pairs:
-            nc.vector.scalar_tensor_tensor(
-                lead[:, pair, :], ratio_v[:, pair, :], RATIO_SCALE, soft_j[:, pair, :], ALU.mult, ALU.subtract
-            )
-        for pair in pairs:
-            nc.vector.scalar_tensor_tensor(
-                base[:, pair, :], gain[:, pair, :], GAIN_SCALE, soft_v[:, pair, :], ALU.mult, ALU.mult
-            )
-
-        mean = [psum.tile([P, P], F32, name="mean%d" % h) for h in range(HALVES)]
+        mean = [psum.tile([P, P], F32, name="mean%d" % h, tag="bank_y0%d" % h) for h in range(HALVES)]
 
         def add_turned(src, t, start, stop):
             for h in range(HALVES):
@@ -199,8 +220,39 @@ def tile_picked_yfarqu_cond_p_kernel(
                     mean[h][:], src[:, t, h * P : (h + 1) * P], ident[:], start=start, stop=stop, is_transpose=True
                 )
 
-        for t in range(D):
-            add_turned(base, t, t == 0, False)
+        def squares(u):
+            for i in range(2):
+                t = 2 * u + i
+                nc.scalar.activation(square[:, t, :], soft_j[u][:, i, :], ACT.Square, bias=centre[:, t : t + 1])
+
+        def roots(u):
+            for t in range(2 * u, 2 * u + 2):
+                nc.scalar.activation(root[:, t, :], square[:, t, :], ACT.Sqrt, bias=floor[:, t : t + 1])
+
+        def ratio_and_base(u):
+            pair = pairs[u]
+            nc.vector.scalar_tensor_tensor(
+                ratio_v[:, pair, :], tanh_a[:, pair, :], RATIO_SHIFT, soft_v[u][:], ALU.add, ALU.mult
+            )
+            nc.vector.scalar_tensor_tensor(
+                base[:, pair, :], gain[:, pair, :], GAIN_SCALE, soft_v[u][:], ALU.mult, ALU.mult
+            )
+            for t in range(pair.start, pair.stop):
+                add_turned(base, t, t == 0, False)
+
+        def leads(u):
+            nc.vector.scalar_tensor_tensor(
+                lead[:, pairs[u], :], ratio_v[:, pairs[u], :], RATIO_SCALE, soft_j[u][:], ALU.mult, ALU.subtract
+            )
+
+        squares(0)
+        ratio_and_base(0)
+        ratio_and_base(1)
+        leads(0)
+        roots(0)
+        leads(1)
+        squares(1)
+        roots(1)
 
         gap = keep.tile([P, D, N], F32, name="gap")
         diff = keep.tile([P, D, N], F32, name="diff")
@@ -216,23 +268,28 @@ def tile_picked_yfarqu_cond_p_kernel(
                 diff[:, pair, :], tanh_b[:, pair, :], 4.0, gap[:, pair, :], ALU.add, ALU.mult
             )
             nc.scalar.activation(size[:, pair, :], diff[:, pair, :], ACT.Abs, scale=DIFF_UNIT)
-        for pair in pairs:
+
+        def subtract_loss(tiles):
             nc.vector.scalar_tensor_tensor(
-                loss[:, pair, :], diff[:, pair, :], 0.0, cut[:, pair, :], ALU.max, ALU.mult
+                loss[:, tiles, :], diff[:, tiles, :], 0.0, cut[:, tiles, :], ALU.max, ALU.mult
             )
-            for t in range(pair.start, pair.stop):
+            for t in range(tiles.start, tiles.stop):
                 add_turned(loss, t, False, t == D - 1)
+
+        subtract_loss(pairs[0])
         for u in range(2):
             nc.vector.tensor_tensor(pair_max[:, u, :], size[:, 2 * u, :], size[:, 2 * u + 1, :], ALU.max)
+        subtract_loss(slice(2, 3))
         worst = keep.tile([P, N], F32, name="worst")
         nc.vector.tensor_tensor(worst[:], pair_max[:, 0, :], pair_max[:, 1, :], ALU.max)
+        weighted = keep.tile([P, HALVES, P], F32, name="weighted")
+        for h in range(HALVES):
+            turned = psum.tile([P, P], F32, name="turned%d" % h, tag="bank_y1%d" % h)
+            nc.tensor.transpose(turned[:], worst[:, h * P : (h + 1) * P], ident[:])
+            nc.scalar.activation(weighted[:, h, :], turned[:], ACT.Copy, scale=wim_col[:, h : h + 1])
+        subtract_loss(slice(3, 4))
 
         result = keep.tile([P, HALVES, P], F32, name="result")
-        mean_sb = keep.tile([P, HALVES, P], F32, name="mean_sb")
         for h in range(HALVES):
-            nc.scalar.copy(mean_sb[:, h, :], mean[h][:])
-            nc.tensor.transpose(yc[h][:, 0, :], worst[:, h * P : (h + 1) * P], ident[:])
-            nc.vector.scalar_tensor_tensor(
-                result[:, h, :], yc[h][:, 0, :], wim_col[:, h : h + 1], mean_sb[:, h, :], ALU.mult, ALU.add
-            )
+            nc.vector.tensor_tensor(result[:, h, :], mean[h][:], weighted[:, h, :], ALU.add)
         nc.sync.dma_start(out.rearrange("(h p) v -> p h v", p=P), result[:])

@@ -50,7 +50,7 @@ def tile_picked_yfarqu_cond_p_kernel(
         nc.sync.dma_start(offsets[:], offs)
 
         scale_table = keep.tile([P, T], U8, name="scale_table", align_bytes=64)
-        nc.gpsimd.memset(scale_table[:].bitcast(I32), 0)
+        nc.vector.memset(scale_table[:].bitcast(I32), 0)
 
         def load_weight(name, columns):
             raw = keep.tile([P, PACK, columns.shape[1]], F32, name=name, tag=name)
@@ -112,17 +112,16 @@ def tile_picked_yfarqu_cond_p_kernel(
                 stop=True,
             )
 
-        yc = [psum.tile([P, D, P], F32, name="yc%d" % h, tag="bank_c%d" % h) for h in range(HALVES)]
         tanh_a = keep.tile([P, D, N], F32, name="tanh_a")
         tanh_b = keep.tile([P, D, N], F32, name="tanh_b")
         tanh_c = keep.tile([P, D, N], F32, name="tanh_c")
-        for h in range(HALVES):
-            for t in range(D):
-                product(yc[h][:, t, :], t, w3_codes[h][:], w3_scales[h][:])
+        for h, tiles, bank in ((0, slice(0, 2), "bank_s0"), (0, slice(2, 4), "bank_c0"), (1, slice(0, 4), "bank_c1")):
+            count = tiles.stop - tiles.start
+            yc = psum.tile([P, count, P], F32, name="yc_" + bank, tag=bank)
+            for i in range(count):
+                product(yc[:, i, :], tiles.start + i, w3_codes[h][:], w3_scales[h][:])
             for dst, half_log in ((tanh_c, HALF_LOG_C), (tanh_a, HALF_LOG_A), (tanh_b, HALF_LOG_B)):
-                nc.scalar.activation(
-                    dst[:, :, h * P : (h + 1) * P], yc[h][:], ACT.Tanh, bias=half_log, scale=0.5
-                )
+                nc.scalar.activation(dst[:, tiles, h * P : (h + 1) * P], yc[:], ACT.Tanh, bias=half_log, scale=0.5)
 
         jv_codes = [keep.tile([P, N], U32, name="jv_codes%d" % b, align_bytes=64) for b in range(2)]
         jv_scales = [keep.tile([P, N], U8, name="jv_scales%d" % b, align_bytes=64) for b in range(2)]
@@ -130,15 +129,6 @@ def tile_picked_yfarqu_cond_p_kernel(
             grouped = keep.tile([P, N, PACK], BF16, name="jv_grouped%d" % i, tag="grouped%d" % (1 - i), align_bytes=64)
             nc.vector.tensor_copy(grouped[:], raw[:].rearrange("p j m -> p m j"))
             quantize(grouped, jv_codes[i][:], jv_scales[i][:])
-
-        centre = keep.tile([P, D], F32, name="centre")
-        lift = keep.tile([P, D], F32, name="lift")
-        light_part = keep.tile([P, D], F32, name="light_part")
-        floor = keep.tile([P, D], F32, name="floor")
-        nc.gpsimd.tensor_scalar(centre[:], light_col[:], -0.2, 0.75 - SHIFT, ALU.mult, ALU.add)
-        nc.gpsimd.tensor_scalar(lift[:], light_col[:], 0.5, 0.75 - SHIFT, ALU.mult, ALU.add)
-        nc.gpsimd.tensor_scalar(light_part[:], light_col[:], 0.21, 0.0, ALU.mult, ALU.add)
-        nc.gpsimd.tensor_tensor(floor[:], light_part[:], light_col[:], ALU.mult)
 
         grown = [keep.tile([P, HALVES, S], F32, name="grown%d" % b) for b in range(2)]
         excess = [keep.tile([P, HALVES, S], F32, name="excess%d" % b) for b in range(2)]
@@ -161,6 +151,32 @@ def tile_picked_yfarqu_cond_p_kernel(
                 )
                 nc.scalar.activation(grown[b][:, h, :], y[b][h][:], ACT.Exp)
 
+        pairs = [slice(0, 2), slice(2, 4)]
+        soft_tags = [["bank_s0", "bank_c0"], ["bank_s1", "bank_c1"]]
+        soft = [
+            [psum.tile([P, 2, N], F32, name="soft%d%d" % (b, u), tag=soft_tags[b][u]) for u in range(2)]
+            for b in range(2)
+        ]
+
+        def turn_into_soft(src, b, h, t, start, stop):
+            nc.tensor.matmul(
+                soft[b][t // 2][:, t % 2, h * P : (h + 1) * P],
+                src[b][:, h, t * P : (t + 1) * P],
+                ident[:],
+                start=start,
+                stop=stop,
+                is_transpose=True,
+            )
+
+        for b in range(2):
+            nc.vector.tensor_scalar_min(grown[b][:], grown[b][:], EXP_CAP)
+            for h in range(HALVES):
+                nc.vector.tensor_scalar(
+                    excess[b][:, h, :], y[b][h][:], -math.log(EXP_CAP), 0.0, ALU.add, ALU.max
+                )
+                for t in range(D):
+                    turn_into_soft(excess, b, h, t, h == 0 and t % 2 == 0, False)
+
         cut = keep.tile([P, D, N], F32, name="cut", tag="w2_raw")
         nc.vector.tensor_scalar(
             cut[:], tanh_c[:], -INV_C_SLOPE * CUT_UNIT, (1.0 / 0.7 - INV_C_SLOPE) * CUT_UNIT, ALU.mult, ALU.add
@@ -168,43 +184,22 @@ def tile_picked_yfarqu_cond_p_kernel(
         gain = keep.tile([P, D, N], F32, name="gain")
         nc.vector.scalar_tensor_tensor(gain[:], tanh_a[:], GAIN_SHIFT, cut[:], ALU.add, ALU.mult)
 
-        pairs = [slice(0, 2), slice(2, 4)]
-        for b in range(2):
-            for h in range(HALVES):
-                nc.vector.tensor_scalar(
-                    excess[b][:, h, :], y[b][h][:], -math.log(EXP_CAP), 0.0, ALU.add, ALU.max
-                )
-            nc.vector.tensor_scalar_min(grown[b][:], grown[b][:], EXP_CAP)
+        centre = keep.tile([P, D], F32, name="centre")
+        lift = keep.tile([P, D], F32, name="lift")
+        floor = keep.tile([P, D], F32, name="floor")
+        nc.vector.tensor_scalar(centre[:], light_col[:], -0.2, 0.75 - SHIFT, ALU.mult, ALU.add)
+        nc.vector.tensor_scalar(lift[:], light_col[:], 0.5, 0.75 - SHIFT, ALU.mult, ALU.add)
+        nc.vector.scalar_tensor_tensor(floor[:], light_col[:], 0.21, light_col[:], ALU.mult, ALU.mult)
 
-        soft_tags = [["bank_s0", "bank_c0"], ["bank_s1", "bank_c1"]]
-        soft = [
-            [psum.tile([P, 2, N], F32, name="soft%d%d" % (b, u), tag=soft_tags[b][u]) for u in range(2)]
-            for b in range(2)
-        ]
-
-        def turn_into_soft(src, b, u, opens):
-            for i in range(2):
-                for h in range(HALVES):
-                    t = 2 * u + i
-                    nc.tensor.matmul(
-                        soft[b][u][:, i, h * P : (h + 1) * P],
-                        src[b][:, h, t * P : (t + 1) * P],
-                        ident[:],
-                        start=opens and i == 0 and h == 0,
-                        stop=(not opens) and i == 1 and h == HALVES - 1,
-                        is_transpose=True,
-                    )
-
-        for b in range(2):
-            for u in range(2):
-                turn_into_soft(excess, b, u, True)
         for u in range(2):
             for b in range(2):
                 columns = slice(2 * u * P, 2 * (u + 1) * P)
                 nc.scalar.activation(
                     logs[b][:, :, columns], grown[b][:, :, columns], ACT.Ln, bias=math.exp(SHIFT), scale=math.exp(SHIFT)
                 )
-                turn_into_soft(logs, b, u, False)
+                for t in range(2 * u, 2 * u + 2):
+                    for h in range(HALVES):
+                        turn_into_soft(logs, b, h, t, False, t % 2 == 1 and h == HALVES - 1)
         soft_v, soft_j = soft
 
         square = keep.tile([P, D, N], F32, name="square")
@@ -212,69 +207,71 @@ def tile_picked_yfarqu_cond_p_kernel(
         ratio_v = keep.tile([P, D, N], F32, name="ratio_v")
         lead = keep.tile([P, D, N], F32, name="lead")
         base = keep.tile([P, D, N], F32, name="base")
-        mean = [psum.tile([P, P], F32, name="mean%d" % h, tag="bank_y0%d" % h) for h in range(HALVES)]
-
-        def add_turned(src, t, start, stop):
-            for h in range(HALVES):
-                nc.tensor.matmul(
-                    mean[h][:], src[:, t, h * P : (h + 1) * P], ident[:], start=start, stop=stop, is_transpose=True
-                )
-
-        def squares(u):
-            for i in range(2):
-                t = 2 * u + i
-                nc.scalar.activation(square[:, t, :], soft_j[u][:, i, :], ACT.Square, bias=centre[:, t : t + 1])
-
-        def roots(u):
-            for t in range(2 * u, 2 * u + 2):
-                nc.scalar.activation(root[:, t, :], square[:, t, :], ACT.Sqrt, bias=floor[:, t : t + 1])
-
-        def ratio_and_base(u):
-            pair = pairs[u]
-            nc.vector.scalar_tensor_tensor(
-                ratio_v[:, pair, :], tanh_a[:, pair, :], RATIO_SHIFT, soft_v[u][:], ALU.add, ALU.mult
-            )
-            nc.vector.scalar_tensor_tensor(
-                base[:, pair, :], gain[:, pair, :], GAIN_SCALE, soft_v[u][:], ALU.mult, ALU.mult
-            )
-            for t in range(pair.start, pair.stop):
-                add_turned(base, t, t == 0, False)
-
-        def leads(u):
-            nc.vector.scalar_tensor_tensor(
-                lead[:, pairs[u], :], ratio_v[:, pairs[u], :], RATIO_SCALE, soft_j[u][:], ALU.mult, ALU.subtract
-            )
-
-        squares(0)
-        ratio_and_base(0)
-        ratio_and_base(1)
-        leads(0)
-        roots(0)
-        leads(1)
-        squares(1)
-        roots(1)
-
         gap = keep.tile([P, D, N], F32, name="gap")
         diff = keep.tile([P, D, N], F32, name="diff")
         loss = keep.tile([P, D, N], F32, name="loss")
         size = keep.tile([P, D, N], F32, name="size")
         pair_max = keep.tile([P, 2, N], F32, name="pair_max")
-        for t in range(D):
+        mean = [psum.tile([P, P], F32, name="mean%d" % h, tag="bank_y0%d" % h) for h in range(HALVES)]
+
+        def add_turned(src, tiles, opens, closes):
+            for t in range(tiles.start, tiles.stop):
+                for h in range(HALVES):
+                    nc.tensor.matmul(
+                        mean[h][:],
+                        src[:, t, h * P : (h + 1) * P],
+                        ident[:],
+                        start=opens and t == 0,
+                        stop=closes and t == D - 1,
+                        is_transpose=True,
+                    )
+
+        def square_of(t):
+            nc.scalar.activation(square[:, t, :], soft_j[t // 2][:, t % 2, :], ACT.Square, bias=centre[:, t : t + 1])
+
+        def root_of(t):
+            nc.scalar.activation(root[:, t, :], square[:, t, :], ACT.Sqrt, bias=floor[:, t : t + 1])
+
+        square_of(0)
+        for u in range(2):
+            nc.vector.scalar_tensor_tensor(
+                ratio_v[:, pairs[u], :], tanh_a[:, pairs[u], :], RATIO_SHIFT, soft_v[u][:], ALU.add, ALU.mult
+            )
+        for u in range(2):
+            nc.vector.scalar_tensor_tensor(
+                lead[:, pairs[u], :], ratio_v[:, pairs[u], :], RATIO_SCALE, soft_j[u][:], ALU.mult, ALU.subtract
+            )
+        root_of(0)
+        for t in range(1, D):
+            square_of(t)
+            root_of(t)
+        for u in range(2):
+            nc.vector.scalar_tensor_tensor(
+                base[:, pairs[u], :], gain[:, pairs[u], :], GAIN_SCALE, soft_v[u][:], ALU.mult, ALU.mult
+            )
+            add_turned(base, pairs[u], True, False)
+
+        def gap_of(t):
             nc.vector.scalar_tensor_tensor(
                 gap[:, t, :], root[:, t, :], lift[:, t : t + 1], lead[:, t, :], ALU.subtract, ALU.add
             )
-        for pair in pairs:
-            nc.vector.scalar_tensor_tensor(
-                diff[:, pair, :], tanh_b[:, pair, :], 4.0, gap[:, pair, :], ALU.add, ALU.mult
-            )
-            nc.scalar.activation(size[:, pair, :], diff[:, pair, :], ACT.Abs, scale=DIFF_UNIT)
+
+        def diff_of(t):
+            nc.vector.scalar_tensor_tensor(diff[:, t, :], tanh_b[:, t, :], 4.0, gap[:, t, :], ALU.add, ALU.mult)
 
         def subtract_loss(tiles):
             nc.vector.scalar_tensor_tensor(
                 loss[:, tiles, :], diff[:, tiles, :], 0.0, cut[:, tiles, :], ALU.max, ALU.mult
             )
-            for t in range(tiles.start, tiles.stop):
-                add_turned(loss, t, False, t == D - 1)
+            add_turned(loss, tiles, False, True)
+
+        gap_of(0)
+        for t in range(1, D):
+            gap_of(t)
+            diff_of(t - 1)
+        diff_of(D - 1)
+        for tiles in (pairs[0], slice(2, 3), slice(3, 4)):
+            nc.scalar.activation(size[:, tiles, :], diff[:, tiles, :], ACT.Abs, scale=DIFF_UNIT)
 
         subtract_loss(pairs[0])
         for u in range(2):
@@ -289,7 +286,7 @@ def tile_picked_yfarqu_cond_p_kernel(
             nc.scalar.activation(weighted[:, h, :], turned[:], ACT.Copy, scale=wim_col[:, h : h + 1])
         subtract_loss(slice(3, 4))
 
-        result = keep.tile([P, HALVES, P], F32, name="result")
-        for h in range(HALVES):
-            nc.vector.tensor_tensor(result[:, h, :], mean[h][:], weighted[:, h, :], ALU.add)
-        nc.sync.dma_start(out.rearrange("(h p) v -> p h v", p=P), result[:])
+        for h, queue in enumerate((nc.sync, nc.scalar)):
+            result = keep.tile([P, P], F32, name="result%d" % h)
+            nc.vector.tensor_tensor(result[:], mean[h][:], weighted[:, h, :], ALU.add)
+            queue.dma_start(out[h * P : (h + 1) * P, :], result[:])

@@ -50,7 +50,7 @@ def tile_picked_yfarqu_cond_p_kernel(
         nc.sync.dma_start(offsets[:], offs)
 
         scale_table = keep.tile([P, T], U8, name="scale_table", align_bytes=64)
-        nc.vector.memset(scale_table[:].bitcast(I32), 0)
+        nc.gpsimd.memset(scale_table[:].bitcast(I32), 0)
 
         def load_weight(name, columns):
             raw = keep.tile([P, PACK, columns.shape[1]], F32, name=name, tag=name)
@@ -169,15 +169,16 @@ def tile_picked_yfarqu_cond_p_kernel(
             )
 
         for b in range(2):
-            nc.vector.tensor_scalar_min(grown[b][:], grown[b][:], EXP_CAP)
             for h in range(HALVES):
+                if h == HALVES - 1:
+                    nc.vector.tensor_scalar_min(grown[b][:], grown[b][:], EXP_CAP)
                 nc.vector.tensor_scalar(
                     excess[b][:, h, :], y[b][h][:], -math.log(EXP_CAP), 0.0, ALU.add, ALU.max
                 )
                 for t in range(D):
                     turn_into_soft(excess, b, h, t, h == 0 and t % 2 == 0, False)
 
-        cut = keep.tile([P, D, N], F32, name="cut", tag="w2_raw")
+        cut = keep.tile([P, D, N], F32, name="cut", tag="grouped0", align_bytes=64)
         nc.vector.tensor_scalar(
             cut[:], tanh_c[:], -INV_C_SLOPE * CUT_UNIT, (1.0 / 0.7 - INV_C_SLOPE) * CUT_UNIT, ALU.mult, ALU.add
         )
@@ -284,7 +285,13 @@ def tile_picked_yfarqu_cond_p_kernel(
             turned = psum.tile([P, P], F32, name="turned%d" % h, tag="bank_y1%d" % h)
             nc.tensor.transpose(turned[:], worst[:, h * P : (h + 1) * P], ident[:])
             nc.scalar.activation(weighted[:, h, :], turned[:], ACT.Copy, scale=wim_col[:, h : h + 1])
-        subtract_loss(slice(3, 4))
+        last = D - 1
+        for h in range(HALVES):
+            columns = slice(h * P, (h + 1) * P)
+            nc.vector.scalar_tensor_tensor(
+                loss[:, last, columns], diff[:, last, columns], 0.0, cut[:, last, columns], ALU.max, ALU.mult
+            )
+            nc.tensor.matmul(mean[h][:], loss[:, last, columns], ident[:], start=False, stop=True, is_transpose=True)
 
         for h, queue in enumerate((nc.sync, nc.scalar)):
             result = keep.tile([P, P], F32, name="result%d" % h)

import math
from contextlib import ExitStack

import concourse.mybir as mybir
from concourse.masks import make_identity

F32 = mybir.dt.float32
BF16 = mybir.dt.bfloat16
I32 = mybir.dt.int32
U32 = mybir.dt.uint32
U16 = mybir.dt.uint16
U8 = mybir.dt.uint8
FP8X4 = mybir.dt.float8_e4m3fn_x4
ACT = mybir.ActivationFunctionType
ALU = mybir.AluOpType

P = 128
K, T, S, D, N = 512, 2048, 512, 4, 256
PACK = 4
HALVES = N // P
FLOPS = 3 * 2 * K * N * S

SLOPE = 0.714286
SHIFT = 0.25
EXP_CAP = 2.0**60
FIRST_WORDS = 512

HALF_LOG_A = 0.5 * math.log(2.3 / 1.1)
HALF_LOG_B = 0.5 * math.log(7.2 / 2.4)
HALF_LOG_C = 0.5 * math.log(1.9 / 0.7)
INV_A_SLOPE = 0.6 / (1.1 * 2.3)
RATIO_SCALE = (0.4 / SLOPE) * 2.0 * INV_A_SLOPE
RATIO_SHIFT = 1.0 + (4.0 - 2.0 / 1.1) / (2.0 * INV_A_SLOPE)
DIFF_UNIT = SLOPE / 12.0
INV_C_SLOPE = 0.6 / (0.7 * 1.9)
CUT_UNIT = -DIFF_UNIT / D
GAIN_SHIFT = 1.0 + (0.95 - 0.8 / 1.1) / (0.8 * INV_A_SLOPE)
GAIN_SCALE = (0.8 / D) * (0.8 * INV_A_SLOPE) / CUT_UNIT


def tile_picked_yfarqu_cond_p_kernel(
    tc, x_words, x_scales, w1, w2, w3, light, wim, offs, out
):
    nc = tc.nc
    with ExitStack() as ctx:
        keep = ctx.enter_context(tc.tile_pool(name="keep", bufs=1))
        psum = ctx.enter_context(tc.psum_pool(name="psum", bufs=1))

        offsets = keep.tile([P, S // 16], U16, name="offsets")
        nc.sync.dma_start(offsets[:], offs)

        scale_table = keep.tile([P, T], U8, name="scale_table", align_bytes=64)
        nc.gpsimd.memset(scale_table[:].bitcast(I32), 0)

        def load_weight(name, columns):
            raw = keep.tile([P, PACK, columns.shape[1]], F32, name=name, tag=name)
            nc.sync.dma_start(raw[:], columns.rearrange("(p j) m -> p j m", j=PACK))
            return raw

        word_table = keep.tile([P, T], I32, name="word_table", align_bytes=64)
        words = x_words[0].rearrange("p c r -> p (c r)").bitcast(I32)
        nc.sync.dma_start(word_table[:, 0:FIRST_WORDS], words[:, 0:FIRST_WORDS])
        for q in range(4):
            nc.sync.dma_start(
                scale_table[32 * q : 32 * q + 4, :].bitcast(I32),
                x_scales[0, 4 * q : 4 * q + 4, :].bitcast(I32),
            )
        nc.sync.dma_start(word_table[:, FIRST_WORDS:T], words[:, FIRST_WORDS:T])
        w3_raw = [load_weight("w3_raw%d" % h, w3[:, h * P : (h + 1) * P]) for h in range(HALVES)]
        w1_raw = load_weight("w1_raw", w1)
        w2_raw = load_weight("w2_raw", w2)
        light_col = keep.tile([P, D], F32, name="light_col")
        nc.sync.dma_start(light_col[:], light[0].rearrange("(p t) -> p t", t=D))
        wim_col = keep.tile([P, HALVES], F32, name="wim_col")
        with nc.allow_non_contiguous_dma(reason="one weight for each output row"):
            nc.sync.dma_start(wim_col[:], wim.rearrange("(h p) o -> p (h o)", p=P))

        ident = keep.tile([P, P], F32, name="ident")
        make_identity(nc, ident[:])

        w3_grouped, w3_codes, w3_scales = [], [], []
        for h in range(HALVES):
            w3_grouped.append(keep.tile([P, P, PACK], BF16, name="w3_grouped%d" % h, tag="grouped%d" % h, align_bytes=64))
            w3_codes.append(keep.tile([P, P], U32, name="w3_codes%d" % h, align_bytes=64))
            w3_scales.append(keep.tile([P, P], U8, name="w3_scales%d" % h, align_bytes=64))
            nc.scalar.copy(w3_grouped[h][:], w3_raw[h][:].rearrange("p j m -> p m j"))

        def quantize(grouped, codes, scales):
            nc.vector.quantize_mx(
                out=codes.bitcast(FP8X4), scales=scales, in_=grouped[:].rearrange("p m j -> p (m j)")
            )

        picked_scales = keep.tile([P, S], U8, name="picked_scales", align_bytes=64)
        nc.vector.tensor_copy(picked_scales[:], scale_table[:].indirect(offsets[:]))
        x_scale = keep.tile([P, D, P], U8, name="x_scale", align_bytes=64)
        nc.vector.tensor_copy(x_scale[:], picked_scales[:].rearrange("q (p t) -> q t p", t=D))
        x_code = keep.tile([P, D, P], U32, name="x_code", align_bytes=64)
        nc.vector.tensor_copy(
            x_code[:].rearrange("q t p -> q p t"), word_table[:].bitcast(U32).indirect(offsets[:])
        )
        for h in range(HALVES):
            quantize(w3_grouped[h], w3_codes[h][:], w3_scales[h][:])

        def product(acc, t, codes, scales):
            nc.tensor.matmul_mx(
                out=acc,
                lhsT=x_code[:, t, :].bitcast(FP8X4),
                lhsT_scale=x_scale[:, t, :],
                rhs=codes.bitcast(FP8X4),
                rhs_scale=scales,
                start=True,
                stop=True,
            )

        tanh_a = keep.tile([P, D, N], F32, name="tanh_a")
        tanh_b = keep.tile([P, D, N], F32, name="tanh_b")
        tanh_c = keep.tile([P, D, N], F32, name="tanh_c")
        for h, tiles, bank in ((0, slice(0, 2), "bank_s0"), (0, slice(2, 4), "bank_c0"), (1, slice(0, 4), "bank_c1")):
            count = tiles.stop - tiles.start
            yc = psum.tile([P, count, P], F32, name="yc_" + bank, tag=bank)
            for i in range(count):
                product(yc[:, i, :], tiles.start + i, w3_codes[h][:], w3_scales[h][:])
            for dst, half_log in ((tanh_c, HALF_LOG_C), (tanh_a, HALF_LOG_A), (tanh_b, HALF_LOG_B)):
                nc.scalar.activation(dst[:, tiles, h * P : (h + 1) * P], yc[:], ACT.Tanh, bias=half_log, scale=0.5)

        jv_codes = [keep.tile([P, N], U32, name="jv_codes%d" % b, align_bytes=64) for b in range(2)]
        jv_scales = [keep.tile([P, N], U8, name="jv_scales%d" % b, align_bytes=64) for b in range(2)]
        for i, raw in enumerate((w1_raw, w2_raw)):
            grouped = keep.tile([P, N, PACK], BF16, name="jv_grouped%d" % i, tag="grouped%d" % (1 - i), align_bytes=64)
            nc.vector.tensor_copy(grouped[:], raw[:].rearrange("p j m -> p m j"))
            quantize(grouped, jv_codes[i][:], jv_scales[i][:])

        grown = [keep.tile([P, HALVES, S], F32, name="grown%d" % b) for b in range(2)]
        excess = [keep.tile([P, HALVES, S], F32, name="excess%d" % b) for b in range(2)]
        logs = [keep.tile([P, HALVES, S], F32, name="logs%d" % b) for b in range(2)]
        y = [
            [psum.tile([P, S], F32, name="y%d%d" % (b, h), tag="bank_y%d%d" % (b, h)) for h in range(HALVES)]
            for b in range(2)
        ]
        for b in range(2):
            for h in range(HALVES):
                columns = slice(h * P, (h + 1) * P)
                nc.tensor.matmul_mx(
                    out=y[b][h][:],
                    lhsT=jv_codes[b][:, columns].bitcast(FP8X4),
                    lhsT_scale=jv_scales[b][:, columns],
                    rhs=x_code[:].rearrange("q t p -> q (t p)").bitcast(FP8X4),
                    rhs_scale=x_scale[:].rearrange("q t p -> q (t p)"),
                    start=True,
                    stop=True,
                )
                nc.scalar.activation(grown[b][:, h, :], y[b][h][:], ACT.Exp)

        pairs = [slice(0, 2), slice(2, 4)]
        soft_tags = [["bank_s0", "bank_c0"], ["bank_s1", "bank_c1"]]
        soft = [
            [psum.tile([P, 2, N], F32, name="soft%d%d" % (b, u), tag=soft_tags[b][u]) for u in range(2)]
            for b in range(2)
        ]

        def turn_into_soft(src, b, h, t, start, stop):
            nc.tensor.matmul(
                soft[b][t // 2][:, t % 2, h * P : (h + 1) * P],
                src[b][:, h, t * P : (t + 1) * P],
                ident[:],
                start=start,
                stop=stop,
                is_transpose=True,
            )

        for b in range(2):
            for h in range(HALVES):
                if h == HALVES - 1:
                    nc.vector.tensor_scalar_min(grown[b][:], grown[b][:], EXP_CAP)
                nc.vector.tensor_scalar(
                    excess[b][:, h, :], y[b][h][:], -math.log(EXP_CAP), 0.0, ALU.add, ALU.max
                )
                for t in range(D):
                    turn_into_soft(excess, b, h, t, h == 0 and t % 2 == 0, False)

        cut = keep.tile([P, D, N], F32, name="cut", tag="grouped0", align_bytes=64)
        nc.vector.tensor_scalar(
            cut[:], tanh_c[:], -INV_C_SLOPE * CUT_UNIT, (1.0 / 0.7 - INV_C_SLOPE) * CUT_UNIT, ALU.mult, ALU.add
        )
        gain = keep.tile([P, D, N], F32, name="gain")
        nc.vector.scalar_tensor_tensor(gain[:], tanh_a[:], GAIN_SHIFT, cut[:], ALU.add, ALU.mult)

        centre = keep.tile([P, D], F32, name="centre")
        lift = keep.tile([P, D], F32, name="lift")
        floor = keep.tile([P, D], F32, name="floor")
        nc.vector.tensor_scalar(centre[:], light_col[:], -0.2, 0.75 - SHIFT, ALU.mult, ALU.add)
        nc.vector.tensor_scalar(lift[:], light_col[:], 0.5, 0.75 - SHIFT, ALU.mult, ALU.add)
        nc.vector.scalar_tensor_tensor(floor[:], light_col[:], 0.21, light_col[:], ALU.mult, ALU.mult)

        for u in range(2):
            for b in range(2):
                columns = slice(2 * u * P, 2 * (u + 1) * P)
                nc.scalar.activation(
                    logs[b][:, :, columns], grown[b][:, :, columns], ACT.Ln, bias=math.exp(SHIFT), scale=math.exp(SHIFT)
                )
                for t in range(2 * u, 2 * u + 2):
                    for h in range(HALVES):
                        turn_into_soft(logs, b, h, t, False, t % 2 == 1 and h == HALVES - 1)
        soft_v, soft_j = soft

        square = keep.tile([P, D, N], F32, name="square")
        root = keep.tile([P, D, N], F32, name="root")
        ratio_v = keep.tile([P, D, N], F32, name="ratio_v")
        lead = keep.tile([P, D, N], F32, name="lead")
        base = keep.tile([P, D, N], F32, name="base")
        gap = keep.tile([P, D, N], F32, name="gap")
        diff = keep.tile([P, D, N], F32, name="diff")
        loss = keep.tile([P, D, N], F32, name="loss")
        size = keep.tile([P, D, N], F32, name="size")
        pair_max = keep.tile([P, 2, N], F32, name="pair_max")
        mean = [psum.tile([P, P], F32, name="mean%d" % h, tag="bank_y0%d" % h) for h in range(HALVES)]

        def add_turned(src, tiles, opens, closes):
            for t in range(tiles.start, tiles.stop):
                for h in range(HALVES):
                    nc.tensor.matmul(
                        mean[h][:],
                        src[:, t, h * P : (h + 1) * P],
                        ident[:],
                        start=opens and t == 0,
                        stop=closes and t == D - 1,
                        is_transpose=True,
                    )

        def square_of(t):
            nc.scalar.activation(square[:, t, :], soft_j[t // 2][:, t % 2, :], ACT.Square, bias=centre[:, t : t + 1])

        def root_of(t):
            nc.scalar.activation(root[:, t, :], square[:, t, :], ACT.Sqrt, bias=floor[:, t : t + 1])

        square_of(0)
        for u in range(2):
            nc.vector.scalar_tensor_tensor(
                ratio_v[:, pairs[u], :], tanh_a[:, pairs[u], :], RATIO_SHIFT, soft_v[u][:], ALU.add, ALU.mult
            )
        for u in range(2):
            nc.vector.scalar_tensor_tensor(
                lead[:, pairs[u], :], ratio_v[:, pairs[u], :], RATIO_SCALE, soft_j[u][:], ALU.mult, ALU.subtract
            )
        root_of(0)
        for t in range(1, D):
            square_of(t)
            root_of(t)
        for u in range(2):
            nc.vector.scalar_tensor_tensor(
                base[:, pairs[u], :], gain[:, pairs[u], :], GAIN_SCALE, soft_v[u][:], ALU.mult, ALU.mult
            )
            add_turned(base, pairs[u], True, False)

        def gap_of(t):
            nc.vector.scalar_tensor_tensor(
                gap[:, t, :], root[:, t, :], lift[:, t : t + 1], lead[:, t, :], ALU.subtract, ALU.add
            )

        def diff_of(t):
            nc.vector.scalar_tensor_tensor(diff[:, t, :], tanh_b[:, t, :], 4.0, gap[:, t, :], ALU.add, ALU.mult)

        def subtract_loss(tiles):
            nc.vector.scalar_tensor_tensor(
                loss[:, tiles, :], diff[:, tiles, :], 0.0, cut[:, tiles, :], ALU.max, ALU.mult
            )
            add_turned(loss, tiles, False, True)

        gap_of(0)
        for t in range(1, D):
            gap_of(t)
            diff_of(t - 1)
        diff_of(D - 1)
        for tiles in (pairs[0], slice(2, 3), slice(3, 4)):
            nc.scalar.activation(size[:, tiles, :], diff[:, tiles, :], ACT.Abs, scale=DIFF_UNIT)

        subtract_loss(pairs[0])
        for u in range(2):
            nc.vector.tensor_tensor(pair_max[:, u, :], size[:, 2 * u, :], size[:, 2 * u + 1, :], ALU.max)
        subtract_loss(slice(2, 3))
        worst = keep.tile([P, N], F32, name="worst")
        nc.vector.tensor_tensor(worst[:], pair_max[:, 0, :], pair_max[:, 1, :], ALU.max)
        weighted = keep.tile([P, HALVES, P], F32, name="weighted")
        for h in range(HALVES):
            turned = psum.tile([P, P], F32, name="turned%d" % h, tag="bank_y1%d" % h)
            nc.tensor.transpose(turned[:], worst[:, h * P : (h + 1) * P], ident[:])
            nc.scalar.activation(weighted[:, h, :], turned[:], ACT.Copy, scale=wim_col[:, h : h + 1])
        last = D - 1
        for h in range(HALVES):
            columns = slice(h * P, (h + 1) * P)
            nc.vector.scalar_tensor_tensor(
                loss[:, last, columns], diff[:, last, columns], 0.0, cut[:, last, columns], ALU.max, ALU.mult
            )
            nc.tensor.matmul(mean[h][:], loss[:, last, columns], ident[:], start=False, stop=True, is_transpose=True)

        for h, queue in enumerate((nc.sync, nc.scalar)):
            result = keep.tile([P, P], F32, name="result%d" % h)
            nc.vector.tensor_tensor(result[:], mean[h][:], weighted[:, h, :], ALU.add)
            queue.dma_start(out[h * P : (h + 1) * P, :], result[:])
